import numpy as np, ml_dtypes
CORES = [2,3,42,43,82,83,122,123]
N = 8
BF = ml_dtypes.bfloat16
W, H, Q, L, V, TH, TH2 = 4096, 128, 32, 4, 8, 2265, 870
J = Q - L + 1
HALF = (J - 1) // 2
B = HALF + L - 1
def which(s, z):
    return np.maximum(1, np.add.reduce((s <= z[:, None, :]).astype(np.int64), axis=1)) - 1
def place(s, c, k, p):
    sk = np.take_along_axis(s, k[:, None, :], 1); ck = np.take_along_axis(c, k[:, None, :], 1)
    return ((p - sk) * (2 * ck + 1) + 37 * ck) & (W - 1)
def pick(x, f):
    return np.take_along_axis(x, f.reshape(8, 1, -1), 2).reshape(8, 16, -1, H)
def seen(x, s, c, z):
    o = (5 * np.arange(H)) & (H - 1); got = []
    for q in range(N):
        so = s[q][..., o]; co = c[q][..., o]
        got.append(pick(x[q], place(so, co, which(so, z[q]), z[q][:, None, :] + np.arange(Q)[None, :, None] - B)))
    return np.stack(got)
def parts(rng):
    span = rng.integers(116, 141, (N, 8, 1, 1))
    x = 128 + np.floor((rng.random((N, 8, 16, W), dtype=np.float32) - 0.5) * span).astype(np.int64)
    tm = 128 + np.floor((rng.random((N, 8, 16, L, H)) - 0.5) * span[..., None]).astype(np.int64)
    s = np.sort(rng.integers(0, W, (N, 8, 16, H)), axis=2); c = rng.integers(0, 1024, (N, 8, 16, H)); z = rng.integers(16, 3001, (N, 8, H))
    return x, s, c, z, tm
def pack(x, s, c, z, tm):
    return {"xl": np.ascontiguousarray(x).reshape(N, 128, W).astype(np.float32).astype(BF), "s0": np.ascontiguousarray(s).reshape(N, 128, H).astype(np.int32),
            "cf": np.ascontiguousarray(c).reshape(N, 128, H).astype(np.int32), "z0": np.ascontiguousarray(z).astype(np.int32),
            "t0": np.ascontiguousarray(tm).reshape(N, 128, L * H).astype(np.float32).astype(BF)}
def setup_inputs(rng):
    return pack(*parts(rng))
def setup_inputs_spread(rng):
    amps = np.array([4, 16, 32, 64, 96, 128])
    x = np.clip(128 + np.floor((2 * rng.random((N, 8, 16, W), dtype=np.float32) - 1) * rng.choice(amps, (N, 8, 1, W))), 0, 255).astype(np.int64)
    tm = np.clip(128 + np.floor((2 * rng.random((N, 8, 16, L, H)) - 1) * rng.choice(amps, (N, 8, 1, L, H))), 0, 255).astype(np.int64)
    s = np.where(rng.random((N, 8, 1, H)) < 0.5, rng.integers(0, W, (N, 8, 16, H)), np.clip(np.floor(np.exp2(12 * rng.random((N, 8, 16, H)))).astype(np.int64) - 1, 0, W - 1))
    c = np.clip(np.floor(np.exp2(10 * rng.random((N, 8, 16, H)))).astype(np.int64) - 1, 0, 1023)
    z = np.where(rng.random((N, 8, H)) < 0.5, rng.integers(16, 3001, (N, 8, H)), np.clip(np.floor(np.exp2(11.6 * rng.random((N, 8, H)))).astype(np.int64), 16, 3000))
    return pack(x, np.sort(s, axis=2), c, z, tm)
def turns(w, u):
    return np.where((u & 1) == 1, 255 - w, w)
def setup_inputs_ends(rng):
    x = 255 * (rng.random((N, 8, 16, W), dtype=np.float32) < 0.125).astype(np.int64); tm = 255 * (rng.random((N, 8, 16, L, H)) < 0.125).astype(np.int64)
    flip = rng.permutation(np.array([0, 0, 1, 1]))
    for g in range(2, 6):
        if flip[g - 2] == 1: x[:, g] = 255 - x[:, g]; tm[:, g] = 255 - tm[:, g]
    nz = rng.integers(0, 17, (N, 8, 1, H)); low = np.where(np.arange(16).reshape(1, 1, 16, 1) < nz, 0, W - 1)
    s = np.where(rng.random((N, 8, 1, H)) < 0.5, low, (W - 1) * rng.integers(0, 2, (N, 8, 16, H))); s[..., 0] = 0; s[..., H - 1] = W - 1
    c = 1023 * rng.integers(0, 2, (N, 8, 16, H)); z = 16 + 2984 * rng.integers(0, 2, (N, 8, H)); z[..., 0] = 16; z[..., H - 1] = 3000
    level = 255 * int(rng.integers(0, 2)); turn = int(rng.integers(0, 2))
    x[:, 7] = level; rec = 255 * rng.integers(0, 2, (N, 1, 1, H)); rec[..., 0] = 255 - level; rec[..., H - 1] = 255 - level; rec[..., 1] = level; rec[..., H - 2] = level; tm[:, 7] = rec
    for q in range(N): x[q, 0] = 255 * ((q + turn) % 2)
    tm[:, 0] = 255 * rng.integers(0, 2, (N, 1, 1, H))
    x[:, 1, :, 0::2] = 0; x[:, 1, :, 1::2] = 255; tm[:, 1] = 255 * rng.integers(0, 2, (N, 1, L, H))
    code = 255 * rng.integers(0, 2, (16, HALF * N))
    for q in range(N): x[q, 6] = code[:, (np.arange(W) - HALF * q) % (HALF * N)]
    s[:, 6] = 0; c[:, 6] = 0
    b = int(rng.integers(0, N)); s[:, 5] = W - 1; c[:, 5] = 1023; z[:, 5] = 3000; z[b, 5] = 16
    u = np.arange(W) - 4300; col = (u * 2047 + 37 * 1023) & (W - 1)
    far = W - 1 + HALF * (V - 1 - (V - 1) // N)
    p = 255 * rng.integers(0, 2, (16, 1)); other = np.where(rng.permutation(16).reshape(16, 1) < 8, 255 - p, p)
    period = HALF * (N - 1); ring = 255 * rng.integers(0, 2, (16, period)); ring[:, int(u[np.argmin(col)]) % period] = (255 - turns(p, far - HALF))[:, 0]
    for d in range(N):
        near = turns(p if d % 2 == 0 else other, u)
        if d == N - 1: near = np.where((u >= -far - HALF) & (u < -far - HALF + L), turns(p, u), near)
        x[(b + d) % N, 5][:, col] = np.where(u < -2600, near, ring[:, (u + HALF * d) % period])
    y = seen(x, s, c, z)
    tm[:, 6] = y[:, 6, :, J - 1:J - 1 + L]; tm[:, 5] = y[:, 5, :, :L]; tm[b, 5] = turns(other, np.arange(L))[:, :, None]
    return pack(x, s, c, z, tm)
def setup_inputs_corners(rng):
    x, s1, c, z, tm = parts(rng); gs = rng.permutation(8)
    x[:, gs[0]] = 120 + (x[:, gs[0]] & 15); x[:, gs[1]] = rng.integers(0, 256, (N, 16, W))
    kind = rng.integers(0, 8, (N, 8, 1, H)); s = np.where(kind == 1, s1[:, :, 5:6], s1); s = np.where(kind == 2, s1[:, :, ::-1], s); s = np.where(kind == 3, W - 1, s)
    s = np.where(kind == 4, np.arange(16).reshape(1, 1, 16, 1), s); s = np.where(kind == 5, rng.permuted(s1, axis=2), s)
    c = np.where(rng.random((N, 8, 16, H)) < 0.3, rng.choice(np.array([0, 1, 511, 512, 1023]), (N, 8, 16, H)), c)
    so = s[..., (5 * np.arange(H)) & (H - 1)]; near = np.take_along_axis(so, rng.integers(0, 16, (N, 8, 1, H)), 2)[:, :, 0]
    z = np.clip(near + rng.choice(np.array([-6, -1, 0, 1, 5, Q - 1, Q, Q + 1]), (N, 8, H)), 16, 3000)
    y = seen(x, s, c, z); j0 = rng.choice(np.array([0, 1, HALF, J - 1]), (N, 8, 1, 1, H)); m = np.take_along_axis(y, j0 + np.arange(L).reshape(1, 1, 1, L, 1), 3)
    tm = np.where(rng.random((N, 8, 1, 1, H)) < 0.6, m, tm)
    tm[:, gs[2]] = 255 * rng.integers(0, 2, (N, 1, L, H)); tm[:, gs[3]] = m[:, gs[3]]
    tm[:, gs[4]] = 255 * rng.integers(0, 2, (N, 1, L, H)); tm[:, gs[4], :, :, H - 1] = m[:, gs[4], :, :, H - 1]
    return pack(x, s, c, z, tm)
def steps(rng):
    b = TH2 // 16; e = rng.integers(-8, 9, 8)
    return b + np.concatenate([e, -e]) + (np.arange(16) < TH2 - 16 * b).astype(np.int64)
def pairs(rng, total, w):
    a = np.zeros(16, np.int64); a[[0, 9]] = (w + 1) // 2; a[[1, 8]] = w // 2
    rest = total - 2 * w; b = rest // 12; e = rng.integers(-8, 9, 6)
    a[[2, 3, 4, 5, 6, 7, 10, 11, 12, 13, 14, 15]] = b + np.concatenate([e, -e]) + (np.arange(12) < rest - 12 * b).astype(np.int64)
    return a
def setup_inputs_edges(rng):
    x, s, c, z, tm = parts(rng)
    for g in range(8):
        if g % 4 == 1: continue
        p0 = rng.integers(50, 71, 16); p1 = p0 + steps(rng); p2 = p1 + steps(rng); p3 = p2 - steps(rng); p3[int(rng.integers(0, 16))] -= 1
        p = np.stack([p0, p1, p2, p3], axis=1)
        for q in range(N): x[q, g] = p[:, (np.arange(W) + int(rng.integers(0, 4))) & 3]
    w = 257 + 4 * int(rng.integers(0, 6)); p0 = rng.integers(20, 61, 16); p1 = p0 + pairs(rng, TH2 + 1, w); p2 = p1 + rng.integers(1, 4, 16); p3 = p2 - pairs(rng, TH2, w + 2)
    p = np.stack([p0, p1, p2, p3], axis=1)
    for q in range(N): x[q, 5] = p[:, (np.arange(W) + int(rng.integers(0, 4))) & 3]
    y = seen(x, s, c, z); dist = rng.choice(np.array([0, TH - 1, TH, TH + 1]), (N, 8, 1, 1, H)); j0 = rng.integers(0, 4, (N, 8, 1, 1, H))
    m = np.take_along_axis(y, j0 + np.arange(L).reshape(1, 1, 1, L, 1), 3); each = dist // (16 * L)
    d = each + (np.arange(16 * L).reshape(1, 1, 16, L, 1) < dist - 16 * L * each)
    sign = np.where(m < 80, -1, np.where(m > 135, 1, 1 - 2 * (np.arange(16).reshape(1, 1, 16, 1, 1) & 1)))
    planted = (np.arange(8) % 4 != 1).reshape(1, 8, 1, 1, 1)
    return pack(x, s, c, z, np.where(planted, m + sign * d, tm))
def check_inputs(d):
    bad = []
    for k, lo, hi in (("xl", 0, 255), ("s0", 0, W - 1), ("cf", 0, 1023), ("z0", 16, 3000), ("t0", 0, 255)):
        a = np.asarray(d[k]).astype(np.float64)
        if not (np.min(a) >= lo and np.max(a) <= hi): bad.append("range of " + k)
        elif np.any(a != np.floor(a)): bad.append("whole numbers in " + k)
    return bad
def reference(xl, s0, cf, z0, t0):
    x = xl.astype(np.int32).reshape(N, 8, 16, W); s = s0.astype(np.int64).reshape(N, 8, 16, H); c = cf.astype(np.int64).reshape(N, 8, 16, H)
    z = z0.astype(np.int64); tm = t0.astype(np.int32).reshape(N, 8, 16, L, H); ties = np.zeros((N, 8), np.int64)
    row = np.arange(16)[None, :, None]; m = np.arange(Q)[None, :, None]
    for t in range(V):
        for r in range(N):
            q = (r + t) % N
            o = ((5 * np.arange(H)[None, :] + ties[r][:, None]) & (H - 1))[:, None, :]
            so = np.take_along_axis(s[q], o, 2); co = np.take_along_axis(c[q], o, 2)
            k = which(so, z[r])
            y = pick(x[q], place(so, co, k, z[r][:, None, :] + m - B))
            e = np.stack([np.add.reduce(np.abs(y[:, :, j:j + L] - tm[r]), axis=(1, 2)) for j in range(J)])
            best = np.argmin(e, axis=0); tie = np.min(e, axis=0) < TH
            so = so + np.where(tie[:, None, :] & (row >= k[:, None, :]), HALF - best[:, None, :], 0)
            np.put_along_axis(s[q], o, so, 2)
            zz = np.where(tie, z[r], np.maximum(z[r] - Q, 0)); k = np.where(tie, k, which(so, zz))
            v = pick(x[q], place(so, co, k, zz[:, None, :] + m))
            over = (np.add.reduce(np.abs(v[:, :, 1:] - v[:, :, :-1]), axis=1) > TH2)[:, L - 1:]
            n = np.where(np.any(over, axis=1), L + np.argmax(over, axis=1), Q)
            tm[r] = np.take_along_axis(v, n[:, None, None, :] - L + np.arange(L)[None, None, :, None], 2)
            z[r] = zz + n - 1
            ties[r] = np.add.reduce(tie.astype(np.int64), axis=1)
    return {"ys": s.reshape(N, 128, H).astype(np.float32), "yz": z.astype(np.float32), "yt": tm.reshape(N, 128, L * H).astype(np.float32).astype(BF)}

from concourse.mybir import AluOpType as A, ActivationFunctionType as F
import math

NV = 8
PAR = {"ns": (3, 3), "ring": ((0,), (1, 2)), "low": {"v": 0, "s": 0, "t": 0}, "g1": ("vs", "ss"), "g2": ("ssss", "svsv"),
       "tp": "vs", "rot": "v", "mix": 2, "win": 0.02, "order": "ba", "ec": "v"}
LAT = 2.6

SCRATCH = {
    "xs": ("sbuf", [128, 4096], "bfloat16"),
    "s0i": ("sbuf", [128, 128], "int32"), "cfi": ("sbuf", [128, 128], "int32"), "z0i": ("sbuf", [128, 128], "int32"),
    "t0s": ("sbuf", [128, 512], "bfloat16"), "ytb": ("sbuf", [128, 512], "bfloat16"),
    "z0f": ("sbuf", [128, 128], "float32"), "ysb": ("sbuf", [128, 128], "float32"),
    "sdo": ("sbuf", [128, 256], "float32"), "sd0": ("sbuf", [128, 256], "float32"), "sd1": ("sbuf", [128, 256], "float32"),
    "zl": ("sbuf", [128, (NV + 1) * 128], "float32"), "zs": ("sbuf", [128, NV * 128], "float32"),
    "tl": ("sbuf", [128, (NV + 1) * 512], "bfloat16"), "ts": ("sbuf", [128, NV * 512], "bfloat16"),
    "cl": ("sbuf", [128, NV * 2], "float32"), "cs": ("sbuf", [128, NV * 2], "float32"),
    "ip": ("sbuf", [128, 16], "int32"), "pc": ("sbuf", [128, 32], "float32"),
    "colf": ("sbuf", [128, 128], "float32"), "colg": ("sbuf", [128, 128], "float32"), "colq": ("sbuf", [128, 128], "float32"),
    "colr": ("sbuf", [128, 128], "float32"), "colp": ("sbuf", [128, 128], "float32"),
    "bof": ("sbuf", [128, 128], "float32"), "boh": ("sbuf", [128, 128], "float16"), "bos": ("sbuf", [128, 128], "float16"), "boe": ("sbuf", [128, 128], "float16"),
    "geb": ("sbuf", [128, 128], "bfloat16"), "tla": ("sbuf", [128, 16], "bfloat16"), "tlb": ("sbuf", [128, 16], "bfloat16"),
    "bob": ("sbuf", [128, 128], "bfloat16"), "bo32": ("sbuf", [128, 128], "bfloat16"),
    "idf": ("sbuf", [128, 128], "float32"), "idb": ("sbuf", [128, 128], "bfloat16"), "idn": ("sbuf", [128, 128], "bfloat16"),
    "ind": ("sbuf", [128, 32], "bfloat16"), "ctp": ("sbuf", [128, 80], "bfloat16"), "ctn": ("sbuf", [128, 80], "bfloat16"),
    "gef": ("sbuf", [128, 128], "float32"), "gem": ("sbuf", [128, 512], "bfloat16"),
    "tlc": ("sbuf", [128, 16], "float32"), "i8": ("sbuf", [128, 8], "float32"),
    "oneb": ("sbuf", [128, 128], "bfloat16"), "m185": ("sbuf", [128, 128], "bfloat16"),
    "rs1": ("sbuf", [128, 128], "float32"), "rs2": ("sbuf", [128, 128], "float32"),
    "rn1": ("sbuf", [128, 128], "float32"), "rn2": ("sbuf", [128, 128], "float32"),
    "tab": ("sbuf", [128, 128], "bfloat16"), "tabw": ("sbuf", [128, 128], "bfloat16"),
    "tmf": ("sbuf", [128, 128], "float32"), "tmg": ("sbuf", [128, 128], "float32"),
    "rb": ("sbuf", [128, 16], "float32"), "ri": ("sbuf", [128, 8], "int32"), "rm": ("sbuf", [128, 8], "int32"), "rl": ("sbuf", [128, 16], "uint16"),
    "rt": ("sbuf", [128, 8], "float32"), "junk": ("sbuf", [128, 64], "float32"),
    "pt": ("psum", [128, 512], "float32"), "ps0": ("psum", [128, 512], "float32"), "ps1": ("psum", [128, 512], "float32"),
    "pv": ("psum", [128, 512], "float32"), "pd0": ("psum", [128, 512], "float32"), "pd1": ("psum", [128, 512], "float32"),
    "pd2": ("psum", [128, 512], "float32"), "pe": ("psum", [128, 8, 16], "float32"),
}
for _b in "01":
    SCRATCH.update({
        "y" + _b: ("sbuf", [128, 2080], "bfloat16"), "v" + _b: ("sbuf", [128, 2048], "bfloat16"),
        "d" + _b: ("sbuf", [128, 8192], "bfloat16"), "st" + _b: ("sbuf", [128, 2048], "bfloat16"),
        "cm" + _b: ("sbuf", [128, 64], "bfloat16"), "xa" + _b: ("sbuf", [128, 64], "float32"), "xd" + _b: ("sbuf", [128, 64], "float16"),
        "zp" + _b: ("sbuf", [128, 64], "float32"), "dz" + _b: ("sbuf", [128, 64], "float32"), "u" + _b: ("sbuf", [128, 64], "float32"),
        "fi" + _b: ("sbuf", [128, 128], "int32"), "fa" + _b: ("sbuf", [128, 128], "int32"), "of" + _b: ("sbuf", [128, 128], "uint16"),
        "k0" + _b: ("sbuf", [128, 128], "float32"), "k1" + _b: ("sbuf", [128, 128], "float32"), "k2" + _b: ("sbuf", [128, 128], "float32"),
        "ki" + _b: ("sbuf", [128, 64], "int32"), "kj" + _b: ("sbuf", [128, 64], "int32"), "kk" + _b: ("sbuf", [128, 64], "float32"),
        "t3" + _b: ("sbuf", [128, 64], "float32"), "zz" + _b: ("sbuf", [128, 64], "float32"),
        "z2" + _b: ("sbuf", [128, 64], "float32"), "z3" + _b: ("sbuf", [128, 64], "float32"),
        "yy" + _b: ("sbuf", [128, 128], "float32"), "n1" + _b: ("sbuf", [128, 128], "bfloat16"), "n2" + _b: ("sbuf", [128, 128], "bfloat16"),
        "tu" + _b: ("sbuf", [128, 16], "uint16"),
    })

MSG = ["z0", "t0", "z1", "t1", "c"]
SEMAPHORES = ["sv", "ss", "st", "sg"] + ["ld%d" % i for i in range(5)] + ["so%d" % i for i in range(5)]
SEMAPHORES += ["a_%s_%d" % (m, t) for m in MSG for t in range(1, NV + 1) if not (m == "c" and t == NV)]
SEMAPHORES += ["l_%s_%d" % (m, t) for m in MSG for t in range(1, NV + 1) if not (m == "c" and t == NV)]

QSEM = {"v": "sv", "s": "ss", "t": "st", "g": "sg"}


def ap(name, lo=None, hi=None, step=1, p=None, raw=None):
    shape = SCRATCH[name][1]
    if lo is None:
        lo, hi = 0, 1
        for n in shape[1:]:
            hi *= n
    return {"n": name, "lo": lo, "hi": hi, "st": step, "p": p, "raw": raw, "off": None}


def ind(name, lo, hi, off):
    return {"n": name, "lo": lo, "hi": hi, "st": 1, "p": None, "raw": None, "off": off}


def resolve(T, a):
    if not isinstance(a, dict):
        return a
    t = T[a["n"]]
    rows = a["p"] if a["p"] is not None else slice(None)
    if a["raw"] is not None:
        r = t[(rows,) + a["raw"]]
    elif len(SCRATCH[a["n"]][1]) == 3:
        r = t[rows]
    else:
        r = t[rows, a["lo"]:a["hi"]:a["st"]] if a["st"] != 1 else t[rows, a["lo"]:a["hi"]]
    if a["off"] is not None:
        return r.indirect(resolve(T, a["off"]))
    return r


def count(a):
    return max(1, len(range(a["lo"], a["hi"], a["st"])))


def meet(a, b):
    if a[0] >= b[1] or b[0] >= a[1]:
        return False
    if a[2] == b[2] and a[2] > 1 and (a[0] - b[0]) % a[2] != 0:
        return False
    return True


def covers(a, b):
    return a[2] == 1 and a[0] <= b[0] and a[1] >= b[1]


def make_plan():
    ops = []
    acc = {}
    bank = {}
    grp = {}

    low = [0]

    def add(eng, call, args, kw, outs, ins, cost, sem=None, inc=1, after=(), group=None, delay=0.0):
        i = len(ops)
        deps = {}

        def need(j, w):
            deps[j] = deps.get(j, False) or w
        for j in after:
            need(j, False)
        for is_w, aps in ((False, ins), (True, outs)):
            for a in aps:
                lst = acc.setdefault(a["n"], [])
                rg = (a["lo"], a["hi"], a["st"])
                psum = SCRATCH[a["n"]][0] == "psum"
                for r, j, w in lst:
                    if (w or is_w) and j != i and meet(r, rg):
                        if psum and eng == "t" and ops[j]["eng"] == "t":
                            continue
                        need(j, True)
                if psum:
                    b = bank.setdefault(a["n"], {})
                    for e, j in b.items():
                        if j == i:
                            continue
                        if e != eng:
                            need(j, True)
                        elif eng == "t" and group is None:
                            need(j, False)
                    if group == "start":
                        if "t" in b:
                            need(b["t"], False)
                        grp[a["n"]] = [i]
                    elif group == "mid":
                        need(grp[a["n"]][0], False)
                        grp[a["n"]].append(i)
                    elif group == "stop":
                        for j in grp[a["n"]]:
                            need(j, False)
        for is_w, aps in ((False, ins), (True, outs)):
            for a in aps:
                lst = acc[a["n"]]
                rg = (a["lo"], a["hi"], a["st"])
                if is_w and group is None:
                    lst[:] = [x for x in lst if x[1] == i or not covers(rg, x[0])]
                else:
                    lst[:] = [x for x in lst if not (x[0] == rg and x[2] == is_w and ops[x[1]]["eng"] == eng and eng in QSEM)] if not is_w else lst
                lst.append((rg, i, is_w))
                if SCRATCH[a["n"]][0] == "psum":
                    bank[a["n"]][eng] = i
        ops.append({"eng": eng, "call": call, "args": args, "kw": kw, "deps": deps, "cost": cost, "sem": sem, "inc": inc, "delay": delay,
                    "low": PAR["low"].get(eng, 0) if low[0] else 0})
        return i

    V = 0.00104
    def tt(o, a, b, op):
        both = SCRATCH[a["n"]][0] == "sbuf" and SCRATCH[b["n"]][0] == "sbuf"
        return add("v", "tensor_tensor", (o, a, b, op), {}, [o], [a, b], 0.01 + V * max(64, count(o) * (2 if both else 1)))

    def ts(o, a, s1, s2, op0, op1=None):
        ins = [a] + [s for s in (s1, s2) if isinstance(s, dict)]
        args = (o, a, s1, s2, op0) if op1 is None else (o, a, s1, s2, op0, op1)
        return add("v", "tensor_scalar", args, {}, [o], ins, 0.01 + V * max(64, count(o)))

    def gcost(n):
        return 0.07 + n * 1.56 * V

    def vcopy(o, a):
        ins = [a] if a["off"] is None else [a, a["off"]]
        c = 0.01 + V * max(64, count(o)) if a["off"] is None else gcost(count(o))
        return add("v", "tensor_copy", (o, a), {}, [o], ins, c)

    def scan(o, d0, d1, init, op0, op1):
        return add("v", "tensor_tensor_scan", (o, d0, d1, init, op0, op1), {}, [o], [d0, d1], 0.01 + V * max(64, count(o)))

    def fill(o, x):
        return add("v", "memset", (o, x), {}, [o], [], 0.01 + V * max(64, count(o)) * 0.5)

    def act(o, a, func, acc_out=None, **kw):
        ins = [a] if a["off"] is None else [a, a["off"]]
        ins += [x for x in kw.values() if isinstance(x, dict)]
        outs = [o]
        if acc_out is not None:
            outs.append(acc_out)
            kw["accum_out"] = acc_out
        c = 0.06 + V * count(o) if a["off"] is None else 0.08 + count(o) * 1.56 * V
        return add("s", "activation", (o, a, func), kw, outs, ins, c)

    def gather(eng, o, a):
        return vcopy(o, a) if eng == "v" else act(o, a, F.Copy)

    def mm(o, l, r, start=True, stop=True, group=None, f32=False):
        m = count(l)
        c = 0.01 + 0.00052 * max(min(64, m), count(r)) * (4 if f32 else 1)
        return add("t", "matmul", (o, l, r, start, stop), {}, [o], [l, r], c, group=group)

    def iota(o, pattern, base, cm, small=True):
        kw = {"allow_small_or_imprecise_dtypes": True} if small else {}
        return add("g", "iota", (o, pattern, base, cm), kw, [o], [], 0.15 + 0.00125 * 2 * count(o))

    def load(o, src, k, us):
        return add("y", "dma_start", (o, ("T", src)), {}, [o], [], 0.08, sem="ld%d" % k, inc=16, delay=us)

    S64 = lambda n, k=0: ap(n, 64 * k, 64 * k + 64)
    K8 = slice(0, 8)

    load(ap("s0i"), "s0", 0, 2.0)
    load(ap("cfi"), "cf", 1, 2.0)
    load(ap("z0i", p=K8), "z0", 2, 2.0)
    load(ap("t0s"), "t0", 3, 2.5)
    load(ap("xs"), "xl", 4, 8.0)
    iota(ap("ip", 0, 1), [[0, 1]], 0, 1, small=False)
    iota(ap("colg"), [[1, 8], [0, 16]], 0, 0)
    iota(ap("colf"), [[1, 128]], 0, 0)
    iota(ap("colq"), [[0, 8], [1, 16]], 0, 0)
    iota(ap("colr"), [[0, 8], [1, 4], [0, 4]], 0, 0)
    iota(ap("colp"), [[0, 64], [1, 2]], 0, 0)
    iota(ap("i8"), [[16, 8]], 0, 0)
    iota(ap("tlc"), [[128, 16]], 0, 0)
    IP = lambda k: ap("ip", k, k + 1)
    PC = lambda k: ap("pc", k, k + 1)
    AND, SHR = A.bitwise_and, A.arith_shift_right
    ts(IP(1), IP(0), 15, None, AND)
    ts(IP(2), IP(0), 4, None, SHR)
    ts(IP(3), IP(0), 1, None, AND)
    vcopy(PC(0), IP(0)); vcopy(PC(1), IP(1)); vcopy(PC(2), IP(2)); vcopy(PC(3), IP(3))
    ts(ap("bof"), ap("colg"), PC(2), None, A.is_equal)
    vcopy(ap("bob"), ap("bof"))
    ts(ap("gef", p=K8), ap("colg", p=K8), ap("pc", 0, 1, p=K8), None, A.is_equal)
    ts(PC(4), PC(1), 1.0, None, A.add)
    ts(PC(5), PC(1), 18.0, None, A.add)
    vcopy(ap("z0f", p=K8), ap("z0i", p=K8))
    tsi8 = ts(ap("rb", 0, 8), ap("i8"), PC(1), None, A.add)
    ts(ap("ri"), ap("rb", 0, 8), 5.0, None, A.mult)
    ts(ap("rm"), ap("ri"), 127, None, AND)
    vcopy(ap("rl", 0, 8), ap("rm"))
    ts(ap("rl", 8, 16), ap("rm"), 128, None, A.add)
    vcopy(ap("sdo", 0, 128), ap("s0i"))
    ts(ap("sdo", 128, 256), ap("cfi"), 2.0, 1.0, A.mult, A.add)
    gather("v", ap("sd0"), ind("sdo", 0, 256, ap("rl")))
    mm(ap("ps0", 0, 128), ap("gef", p=K8), ap("z0f", p=K8), f32=True)
    vcopy(ap("zl", 0, 128), ap("ps0", 0, 128))
    ts(ap("boh"), ap("bof"), 0.5, None, A.mult)
    ts(ap("bos"), ap("bof"), 16.5, None, A.mult)
    vcopy(ap("boe"), ap("bof"))
    vcopy(ap("geb", p=K8), ap("gef", p=K8))
    fill(ap("oneb"), 1.0)
    fill(ap("m185"), -18.5)
    for b in range(2):
        for a in range(4):
            act(ap("tl", b * 256 + a, b * 256 + 256, 4), ap("t0s", a * 128 + b * 64, a * 128 + b * 64 + 64), F.Copy)
    ts(ap("idf"), ap("colf"), PC(0), None, A.is_equal)
    vcopy(ap("idb"), ap("idf"))
    ts(ap("idn"), ap("idf"), -1.0, None, A.mult)
    ts(ap("bo32"), ap("bof"), 32.0, None, A.mult)
    for k, w in ((0, -64.0), (1, 64.0), (2, 1.0), (3, 32.0)):
        ts(ap("ind", 8 * k, 8 * k + 8), ap("colf", 0, 8), PC(2), w, A.is_equal, A.mult)
    CT = {1: 0, 2: 8, 3: 24, 4: 48}
    for n in (1, 2, 3, 4):
        for r in range(n):
            ts(ap("ctp", CT[n] + r, CT[n] + 8 * n, n), ap("colf", 0, 8), PC(2), 32.0, A.is_equal, A.mult)
    ts(ap("ctn"), ap("ctp"), -1.0, None, A.mult)
    ts(PC(6), PC(3), 16.0, -14.0, A.mult, A.add)
    ts(PC(7), PC(3), 2097152.0, None, A.mult)
    ts(ap("tmf"), ap("colq"), PC(6), None, A.add)
    ts(ap("tmg"), ap("colq"), 13.0, PC(7), A.is_ge, A.mult)
    tt(ap("tab"), ap("tmf"), ap("tmg"), A.add)
    ts(PC(8), PC(3), 32768.0, -32768.0, A.mult, A.add)
    ts(ap("tabw"), ap("colq"), 4.0, PC(8), A.is_lt, A.mult)
    ts(PC(9), PC(3), -48.0, 64.0, A.mult, A.add)
    ts(ap("yy0"), ap("colq"), 0.0, 2e9, A.is_equal, A.mult)
    ts(ap("rs1"), ap("yy0"), -1e9, None, A.add)
    ts(ap("rs2", p=K8), ap("colp", p=K8), -2e9, 1e9, A.mult, A.add)
    ts(ap("tmf"), ap("colq"), 0.0, 1001.0, A.is_equal, A.mult)
    ts(ap("rn1"), ap("tmf"), -1.0, None, A.add)
    ts(ap("rn2", p=K8), ap("colp", p=K8), -1016.0, 1000.0, A.mult, A.add)
    for r in range(4):
        ts(ap("tmg", p=K8), ap("colr", p=K8), float(r), None, A.is_equal)
        tt(ap("gem", 128 * r, 128 * r + 128, p=K8), ap("gef", p=K8), ap("tmg", p=K8), A.mult)
    ts(IP(4), IP(1), 2, None, SHR)
    ts(IP(5), IP(1), 3, None, AND)
    vcopy(PC(10), IP(4)); vcopy(PC(11), IP(5))
    ts(PC(15), PC(10), 32.0, PC(11), A.mult, A.add)
    ts(PC(12), PC(15), 27.0, None, A.add)
    vcopy(ap("tla"), ap("tlc"))
    ts(ap("tlb"), ap("tlc"), 0.0, PC(12), A.mult, A.add)
    for b in "01":
        fill(ap("y" + b, 2048, 2080), 0.0)
        fill(ap("d" + b, 13 * 512, 8192), 0.0)
        fill(ap("st" + b), 0.0)

    def choose(b, z, sd, zcol, first, between=None):
        B = str(b)
        P = "ps" + B
        Sx, Dx = ap(sd, 64 * b, 64 * b + 64), ap(sd, 128 + 64 * b, 192 + 64 * b)
        oh, ge = ap("pv", 256 * b, 256 * b + 64), ap("pv", 256 * b + 64, 256 * b + 128)
        tt(ap("cm" + B), Sx, z, A.is_le)
        mm(ap(P, 0, 64), ap("bob"), ap("cm" + B))
        act(ap("zp" + B), z, F.Identity, bias=zcol)
        if between is not None:
            between()
        ts(oh, ap(P, 0, 64), 1.0, PC(4), A.max, A.is_equal)
        if first:
            ts(ge, ap(P, 0, 64), 1.0, PC(4), A.max, A.is_le)
        tt(ap("xa" + B), oh, Sx, A.mult)
        tt(ap("xd" + B), oh, Dx, A.mult)
        mm(ap(P, 64, 128), ap("bof"), ap("xa" + B), f32=True)
        mm(ap(P, 128, 192), ap("boe"), ap("xd" + B))
        mm(ap(P, 192, 320), ap("oneb", p=slice(0, 1)), ap("m185", p=slice(0, 1)), True, False)
        mm(ap(P, 192, 256), ap("boh"), ap("xd" + B), False, False)
        mm(ap(P, 256, 320), ap("bos"), ap("xd" + B), False, True)
        tt(ap("dz" + B), ap("zp" + B), ap(P, 64, 128), A.subtract)
        tt(ap("u" + B), ap("dz" + B), ap(P, 128, 192), A.mult)
        tt(ap("fi" + B, 0, 128, 2), ap("u" + B), ap(P, 192, 256), A.add)
        tt(ap("fi" + B, 1, 128, 2), ap("u" + B), ap(P, 256, 320), A.add)
        ts(ap("fa" + B), ap("fi" + B), 4095, None, AND)
        vcopy(ap("of" + B), ap("fa" + B))

    def cut(b, out, engs):
        n = len(engs)
        for k, e in enumerate(engs):
            w = 2048 // n
            gather(e, ap(out + str(b), k * w, k * w + w), ind("xs", 0, 4096, ap("of" + str(b), k * w // 16, (k + 1) * w // 16)))

    ring = [0, 0]

    def pd(kind):
        ring[kind] += 1
        own = PAR["ring"][kind]
        return "pd%d" % own[ring[kind] % len(own)]

    sends, recvs = {}, {}

    def send(m, t, dst, src):
        sends[(m, t)] = add("g", "send", (dst, src, m, t), {}, [], [src], 0.5)

    def recv(m, t, o):
        after = [sends[(m, t)]]
        recvs[(m, t)] = add("rx", "recv", (m, t), {}, [o], [], 0.0, sem="a_%s_%d" % (m, t), after=after, delay=LAT)

    ZL = lambda t, b: ap("zl", t * 128 + b * 64, t * 128 + b * 64 + 64)
    TLB = lambda t, b: t * 512 + b * 256

    for t in range(NV):
        sd = "sd%d" % (t % 2)
        if t:
            for m in ("z0", "t0", "c", "z1", "t1"):
                if m == "c":
                    recv(m, t, ap("cl", 2 * t, 2 * t + 2))
                elif m[0] == "z":
                    recv(m, t, ZL(t, int(m[1])))
                else:
                    o = TLB(t, int(m[1]))
                    recv(m, t, ap("tl", o, o + 256))
            ca, cb = ap("cl", 2 * t, 2 * t + 1), ap("cl", 2 * t + 1, 2 * t + 2)
            old, new = ap("rb", 8 * ((t + 1) % 2), 8 * ((t + 1) % 2) + 8), ap("rb", 8 * (t % 2), 8 * (t % 2) + 8)
            ts(ap("ri"), old, ca, cb, A.add, A.add)
            ts(ap("rm"), ap("ri"), 127, None, AND)
            vcopy(ap("rl", 0, 8), ap("rm"))
            ts(ap("rl", 8, 16), ap("rm"), 128, None, A.add)
            gather(PAR["rot"], ap(sd), ind("sd%d" % ((t + 1) % 2), 0, 256, ap("rl")))
            low[0] = 1
            ts(ap("rt"), ap("i8"), ca, cb, A.subtract, A.subtract)
            ts(new, ap("rt"), PC(1), None, A.add)
            low[0] = 0
        Sx = lambda b: ap(sd, 64 * b, 64 * b + 64)

        def match(b):
            choose(b, ZL(t, b), sd, PC(4), True)
            cut(b, "y", PAR["g1"][b])

        def distances(b):
            NS = PAR["ns"][b]
            B = str(b)
            o = TLB(t, b)
            Y, D = "y" + B, "d" + B
            Ta = lambda a: ap("tl", o + a, o + 256, 4)
            for a in range(4):
                for h in range(2):
                    mm(ap("pt", a * 128 + h, a * 128 + 128, 2), ap("idb"), Ta(a))
            mm(ap("pe"), ap("idb"), ap("tab"), True, False, group="start")

            def sums(q, a, last=False):
                k = 8 if q < NS else 0
                c = q * 512 + a * 128
                mm(ap("pe", raw=(slice(None), q)), ap(D, c, c + 128), ap("ind", k, k + 8), False, last, group="stop" if last else "mid")

            def corr(m):
                for lo, hi, tabn in ((0, NS, "ctn"), (NS, 16, "ctp")):
                    q0, q1 = max(lo, m - 3), min(hi, m + 1, 16)
                    if q0 < q1:
                        n = q1 - q0
                        mm(ap("pe", raw=(slice(None), slice(q0, q1))), ap(Y, m, m + 16 * 127 + 1, 16), ap(tabn, CT[n], CT[n] + 8 * n), False, False, group="mid")
            low[0] = 1
            order = []
            vq = [q for q in range(NS, 16)]
            sq = list(range(NS))
            while vq or sq:
                if sq:
                    order.append(sq.pop(0))
                order += vq[:PAR["mix"]]
                vq = vq[PAR["mix"]:]
            for q in order:
                if q < NS:
                    R = pd(0)
                    for a in range(4):
                        mm(ap(R, a * 128, a * 128 + 128), ap("idb"), ap(Y, q + a, q + a + 16 * 127 + 1, 16), True, False)
                        mm(ap(R, a * 128, a * 128 + 128, 2), ap("idn"), Ta(a), False, False)
                        mm(ap(R, a * 128 + 1, a * 128 + 128, 2), ap("idn"), Ta(a), False, True)
                    act(ap(D, q * 512, q * 512 + 512), ap(R), F.Relu)
                else:
                    for a in range(4):
                        m, c = q + a, q * 512 + a * 128
                        if q <= 12:
                            tt(ap(D, c, c + 128), ap(Y, m, m + 16 * 127 + 1, 16), ap("pt", a * 128, a * 128 + 128), A.min)
                        else:
                            tt(ap(D, c, c + 128, 2), ap(Y, m, m + 32 * 63 + 1, 32), ap("pt", a * 128, a * 128 + 128, 2), A.min)
            for m in range(19):
                corr(m)
            for k, q in enumerate(order):
                for a in range(4):
                    sums(q, a, k == 15 and a == 3)
            low[0] = 0

        def decide(b):
            B = str(b)
            P = "ps" + B
            o = TLB(t, b)
            K = ap(P, 448, 512)
            if PAR["ec"] == "v":
                vcopy(ap("k0" + B), ap("pe"))
            else:
                act(ap("k0" + B), ap("pe"), F.Copy)
            scan(ap("k1" + B), ap("rs1"), ap("k0" + B), 1e9, A.max, A.min)
            mm(ap(P, 320, 448, p=K8), ap("k1" + B, 15, 128, 16), ap("idf"), f32=True)
            scan(ap("k2" + B, p=K8), ap("rs2", p=K8), ap(P, 320, 448, p=K8), 1e9, A.max, A.min)
            for a in range(4):
                mm(K, ap("bo32"), ap("tl", o + a, o + 256, 4), a == 0, False)
            mm(K, ap("gef", p=K8), ap("k2" + B, 1, 128, 2, p=K8), False, True, f32=True)
            ts(ap("t3" + B), K, 72464.0, 32.0, A.is_lt, A.mult)
            tt(ap("zz" + B), ZL(t, b), ap("t3" + B), A.add)
            act(ap("z2" + B), ap("zz" + B), F.Relu, bias=ap("pc", 13, 14))
            if t < NV - 1:
                act(ap("junk"), ap("t3" + B), F.Copy, scale=77.0 / 32.0, acc_out=ap("cs", 2 * t + b, 2 * t + b + 1))
                if b == 1:
                    send("c", t + 1, ap("cl", 2 * t + 2, 2 * t + 4), ap("cs", 2 * t, 2 * t + 2))

            def starts():
                g0 = 256 * b
                ge, gt, md = ap("pv", g0 + 64, g0 + 128), ap("pv", g0 + 128, g0 + 192), ap("pv", g0 + 192, g0 + 256)
                ts(ap("ki" + B), K, 14.0, None, A.add)
                ts(ap("kj" + B), ap("ki" + B), 31, None, AND)
                tt(gt, ge, ap("t3" + B), A.mult)
                ts(ap("kk" + B), ap("kj" + B), -14.0, 0.03125, A.add, A.mult)
                tt(md, ap("kk" + B), gt, A.mult)
                tt(Sx(b), Sx(b), md, A.subtract)
            choose(b, ap("z2" + B), sd, PC(5), False, starts)
            act(ap("z3" + B), ap("z2" + B), F.Identity, bias=ap("pc", 14, 15))
            cut(b, "v", PAR["g2"][b])

        def renew(b):
            B = str(b)
            P = "ps" + B
            W = ap(P, 64, 192)
            for c in range(4):
                R = pd(1)
                mm(ap(R, 0, 508), ap("idb"), ap("v" + B, 512 * c + 4, 512 * c + 512), True, False)
                mm(ap(R, 0, 508), ap("idn"), ap("v" + B, 512 * c + 3, 512 * c + 511), False, True)
                act(ap("st" + B, 512 * c + 4, 512 * c + 512), ap(R, 0, 508), F.Abs)
            mm(W, ap("idb"), ap("tabw"), True, False)
            for c in range(16):
                mm(ap(P, 64 + c, 192, 16), ap("st" + B, c, 2048, 16), ap("ind", 16, 24), False, c == 15)
            ts(ap("yy" + B), W, 870.5, PC(9), A.is_lt, A.mult)
            scan(ap("n1" + B), ap("rn1"), ap("yy" + B), 0.0, A.add, A.min)
            mm(ap(P, 320, 448, p=K8), ap("n1" + B, 15, 128, 16), ap("idb"))
            scan(ap("n2" + B, p=K8), ap("rn2", p=K8), ap(P, 320, 448, p=K8), 0.0, A.add, A.min)
            mm(ap(P, 0, 16), ap("idb"), ap("tla"), True, False)
            mm(ap(P, 0, 16), ap("idb"), ap("tlb"), False, False)
            for r in range(4):
                mm(ap(P, 0, 16), ap("gem", 128 * r, 128 * r + 128, p=K8), ap("n2" + B, 2 * r + 1, 128, 8, p=K8), False, r == 3)
            mm(ap(P, 448, 512), ap("geb", p=K8), ap("n2" + B, 1, 128, 2, p=K8))
            vcopy(ap("tu" + B), ap(P, 0, 16))
            zo = t * 128 + b * 64
            tt(ap("zs", zo, zo + 64), ap("z3" + B), ap(P, 448, 512), A.add)
            send("z" + B, t + 1, ZL(t + 1, b), ap("zs", zo, zo + 64))
            o = t * 512 + b * 256
            gather(PAR["tp"][b], ap("ts", o, o + 256), ind("v" + B, 0, 2048, ap("tu" + B)))
            send("t" + B, t + 1, ap("tl", o + 512, o + 768), ap("ts", o, o + 256))

        match(0)
        match(1)
        distances(0)
        decide(0)
        if PAR["order"] == "ab":
            distances(1)
            renew(0)
        else:
            renew(0)
            distances(1)
        decide(1)
        if t == NV - 1:
            ca, cb = ap("cl", 2 * t, 2 * t + 1), ap("cl", 2 * t + 1, 2 * t + 2)
            ts(ap("tmf", 0, 8), ap("i8"), PC(1), 77.0, A.add, A.mult)
            ts(ap("ri"), ap("tmf", 0, 8), ca, cb, A.subtract, A.subtract)
            ts(ap("rm"), ap("ri"), 127, None, AND)
            vcopy(ap("rl", 0, 8), ap("rm"))
            gather("v", ap("ysb"), ind(sd, 0, 128, ap("rl", 0, 8)))
            add("y", "dma_start", (("T", "ys"), ap("ysb")), {}, [], [ap("ysb")], 0.08, sem="so0", inc=16, delay=2.0)
        renew(1)
    for b in range(2):
        recv("z%d" % b, NV, ZL(NV, b))
        recv("t%d" % b, NV, ap("tl", TLB(NV, b), TLB(NV, b) + 256))
        add("y", "dma_start", (("C", "yz", 64 * b, 64 * b + 64), ap("zl", NV * 128 + 64 * b, NV * 128 + 64 * b + 64, p=slice(0, 128, 16))), {}, [],
            [ZL(NV, b)], 0.08, sem="so%d" % (1 + b), inc=16, delay=2.0)
        for a in range(4):
            o, i = ap("ytb", a * 128 + b * 64, a * 128 + b * 64 + 64), ap("tl", TLB(NV, b) + a, TLB(NV, b) + 256, 4)
            if a % 2:
                vcopy(o, i)
            else:
                act(o, i, F.Copy)
    add("y", "dma_start", (("T", "yt"), ap("ytb")), {}, [], [ap("ytb")], 0.08, sem="so3", inc=16, delay=2.0)

    n = len(ops)
    succ = [[] for _ in range(n)]
    for i, o in enumerate(ops):
        for j in o["deps"]:
            succ[j].append(i)
    HOP = 0.06
    rank = [0.0] * n
    for i in range(n - 1, -1, -1):
        o = ops[i]
        rank[i] = o["cost"] + o["delay"] + max([HOP + rank[k] for k in succ[i]], default=0.0)
    left = [len(o["deps"]) for o in ops]
    ready = {}
    est = [0.0] * n
    fin = [0.0] * n
    free = {}
    order = []
    for i, o in enumerate(ops):
        if left[i] == 0:
            ready.setdefault(o["eng"], []).append(i)
    while len(order) < n:
        best = None
        for e, lst in ready.items():
            if not lst:
                continue
            f = free.get(e, 0.0)
            t0 = min(max(f, est[i]) for i in lst)
            if best is None or t0 < best[0]:
                best = (t0, e)
        t0, e = best
        lst = ready[e]
        f = free.get(e, 0.0)
        c = [i for i in lst if max(f, est[i]) <= t0 + PAR["win"]]
        i = max(c, key=lambda k: (-ops[k]["low"], rank[k], -k))
        lst.remove(i)
        o = ops[i]
        start = max(f, est[i])
        o["start"] = start
        if e != "rx":
            free[e] = start + o["cost"]
        fin[i] = start + o["cost"] + o["delay"]
        order.append(i)
        for k in succ[i]:
            w = ops[k]["deps"][i]
            est[k] = max(est[k], fin[i] + HOP if w else start + o["cost"])
            left[k] -= 1
            if left[k] == 0:
                ready.setdefault(ops[k]["eng"], []).append(k)
    return ops, order, fin


_PLAN = []


def rank_program(g, core, T, topo):
    rank = T.rank_of(core)
    if rank is None:
        return
    if not _PLAN:
        _PLAN.append(make_plan())
    ops, order, _ = _PLAN[0]
    q = {"v": g.vector, "s": g.scalar, "t": g.tensor, "g": g, "y": g.sync}
    ncore = len(T.cores)
    nxt, prv = T.cores[(rank + 1) % ncore], T.cores[(rank - 1) % ncore]
    off_chip = lambda a, b: topo.chip(a) != topo.chip(b)

    def engines(src, dst):
        return topo.engines(src, dst)[:8]
    mask = 0
    for e in engines(core, nxt):
        mask |= 1 << e
    n_out, n_in = len(engines(core, nxt)), len(engines(prv, core))
    rid, pid = topo.addr(nxt)[0], topo.addr(nxt)[1]

    def res(a):
        if isinstance(a, tuple) and a and a[0] == "T":
            return T[a[1]][:]
        if isinstance(a, tuple) and a and a[0] == "C":
            return T[a[1]][:, a[2]:a[3]]
        return resolve(T, a)
    g_seen = {e: {} for e in q}
    total = {}
    done = [None] * len(ops)
    total["sv"] = 2
    q["v"].memset(T.pc[:, 13:14], -32.0).then_inc(T.sem.sv, 1)
    q["v"].memset(T.pc[:, 14:15], 30.0).then_inc(T.sem.sv, 1)
    q["s"].wait_ge(T.sem.sv, 2)
    g_seen["v"]["sv"] = 0
    g_seen["s"]["sv"] = 2
    for i in order:
        o = ops[i]
        e = o["eng"]
        if e == "rx":
            sem = o["sem"]
            done[i] = (sem, n_in, {sem: n_in})
            total[sem] = n_in
            continue
        seen = g_seen[e]
        for j in sorted(o["deps"], reverse=True):
            if not o["deps"][j]:
                continue
            sem, val, know = done[j]
            if seen.get(sem, 0) < val:
                q[e].wait_ge(T.sem[sem], val)
                for s, c in know.items():
                    if seen.get(s, 0) < c:
                        seen[s] = c
        if o["call"] == "send":
            dst, src, m, t = o["args"]
            g.remote_dma(res(dst), res(src), T.sem["a_%s_%d" % (m, t)], T.sem["l_%s_%d" % (m, t)], pid, rid, mask)
            total["l_%s_%d" % (m, t)] = n_out
            continue
        args = tuple(res(a) for a in o["args"])
        kw = {k: res(x) for k, x in o["kw"].items()}
        if o["call"] == "tensor_tensor":
            ins = q[e].tensor_tensor(*args)
        elif o["call"] == "tensor_scalar":
            ins = q[e].tensor_scalar(*args)
        elif o["call"] == "tensor_copy":
            ins = q[e].tensor_copy(*args)
        elif o["call"] == "tensor_tensor_scan":
            ins = q[e].tensor_tensor_scan(*args)
        elif o["call"] == "memset":
            ins = q[e].memset(*args)
        elif o["call"] == "activation":
            ins = q[e].activation(*args, **kw)
        elif o["call"] == "matmul":
            ins = q[e].matmul(*args)
        elif o["call"] == "iota":
            ins = g.iota(*args, **kw)
        else:
            ins = q[e].dma_start(*args)
        sem = o["sem"] or QSEM[e]
        ins.then_inc(T.sem[sem], o["inc"])
        total[sem] = total.get(sem, 0) + o["inc"]
        know = dict(seen)
        know[sem] = total[sem]
        done[i] = (sem, total[sem], know)
    for sem, val in total.items():
        if g_seen["y"].get(sem, 0) < val:
            q["y"].wait_ge(T.sem[sem], val)
